import numpy as np
import ml_dtypes


def mxq(x, axis, fmt="e4m3"):
    dtype, down = {"e4m3": (ml_dtypes.float8_e4m3fn, 7), "e5m2": (ml_dtypes.float8_e5m2, 14)}[fmt]
    v = np.moveaxis(np.asarray(x, np.float32).astype(ml_dtypes.bfloat16).astype(np.float64), axis, -1)
    blocks = v.reshape(v.shape[:-1] + (-1, 32))
    amax = np.abs(blocks).max(-1, keepdims=True)
    byte = np.maximum(np.where(amax > 0, np.frexp(amax)[1] - 1 + 127, 0) - down, 1)
    scale = np.exp2(byte - 127.0)
    codes = (blocks / scale).astype(np.float32).astype(dtype).astype(np.float64)
    return np.moveaxis((codes * scale).reshape(v.shape), -1, axis)


WIDE = False


def mx_kscale(k, group=512):
    if not WIDE:
        return np.ones(k)
    levels = np.array([18, -18])
    if group != 512:
        return np.exp2(np.random.permutation(np.resize(levels, k // group))).repeat(group)
    if k % 512:
        return np.exp2(np.random.permutation(np.resize(levels, k // 32))).repeat(32)
    a = np.empty((k // 512, 16))
    for p in range(k // 512):
        a[p, :8] = np.random.permutation(np.resize(levels, 8))
        for g in range(8):
            far = levels[np.abs(levels - a[p, g]) >= 10]
            a[p, g + 8] = far[np.random.randint(len(far))]
    return np.exp2(a.ravel()).repeat(32)


def f64(x):
    return np.asarray(x).astype(np.float64)


G, D, M, N = 4, 128, 256, 1024


def setup_inputs():
    n = np.random.standard_normal
    s = mx_kscale(D, 0)[:, None]
    return {
        "x": (n((G, D, N)) * s).astype(np.float32),
        "w": (n((G, D, M)) / np.sqrt(D) / s).astype(np.float32),
    }


def reference(x, w):
    xq = mxq(f64(x), 1, "e4m3")
    y = mxq(f64(w), 1, "e4m3").transpose(0, 2, 1) @ xq
    y = np.maximum(y, 0.0)
    return y

from contextlib import ExitStack

import concourse.mybir as mybir

G, D, M, N = 4, 128, 256, 1024
FLOPS = 2 * G * D * M * N

F32 = mybir.dt.float32
BF16 = mybir.dt.bfloat16
U32 = mybir.dt.uint32
U8 = mybir.dt.uint8
FP8X4 = mybir.dt.float8_e4m3fn_x4
RELU = mybir.ActivationFunctionType.Relu

P = 128
PACK = 4
ROWS = D // PACK
M_TILE = 128
N_TILE = 128
BANK = 512
RUN = 4


def tile_rows_glin_relu_kernel(tc, x, w, out):
    nc = tc.nc
    x_rows = x.rearrange("g (p j) n -> (g p) j n", j=PACK)
    w_rows = w.rearrange("g (p j) m -> (g p) j m", j=PACK)
    out_rows = out.rearrange("g (t s) n -> s (g t) n", s=M_TILE)

    with ExitStack() as ctx:
        sb = ctx.enter_context(tc.tile_pool(name="sb", bufs=1))
        psum = ctx.enter_context(tc.psum_pool(name="psum", bufs=1))
        ctx.enter_context(tc.manual_schedule())

        def load(name, rows):
            raw = sb.tile([P, PACK, rows.shape[2]], F32, name=name)
            nc.sync.dma_start(out=raw[:], in_=rows)
            return raw

        def interleave(name, copy, raw, c0, width):
            grouped = sb.tile([P, width, PACK], BF16, name=name, align_bytes=64)
            copy(
                out=grouped[:].rearrange("p (c i) j -> p c j i", i=RUN),
                in_=raw[:, :, c0 : c0 + width].rearrange("p j (c i) -> p c j i", i=RUN),
            )
            return grouped

        def quantize(name, grouped):
            width = grouped.shape[1]
            codes = sb.tile([P, width], U32, name=name + "_codes", align_bytes=64)
            scales = sb.tile([P, width], U8, name=name + "_scales", align_bytes=64)
            nc.vector.quantize_mx(
                out=codes[:].bitcast(FP8X4),
                scales=scales[:],
                in_=grouped[:].rearrange("p c j -> p (c j)"),
            )
            return codes, scales

        banks = [[psum.tile([P, BANK], F32, name="bank_%d_%d" % (g, s)) for s in range(2)] for g in range(G)]

        def multiply(wq, xq, xc0, g, t, dest):
            rows = slice(ROWS * g, ROWS * (g + 1))
            mc = slice(M_TILE * t, M_TILE * (t + 1))
            xc = slice(xc0, xc0 + N_TILE)
            nc.tensor.matmul_mx(
                out=dest,
                lhsT=wq[0][rows, mc].bitcast(FP8X4),
                lhsT_scale=wq[1][rows, mc],
                rhs=xq[0][rows, xc].bitcast(FP8X4),
                rhs_scale=xq[1][rows, xc],
                start=True,
                stop=True,
            )

        seed = sb.tile([P, 8], F32, name="seed")
        zero = sb.tile([P, 8], F32, name="zero")
        nc.vector.memset(seed[:], 0.0)
        nc.scalar.activation(out=zero[:], in_=seed[:], func=RELU)

        def relu_scalar(dest, bank):
            nc.scalar.activation(out=dest, in_=bank, func=RELU, bias=zero[:, 0:1])

        def relu_vector(dest, bank):
            nc.vector.tensor_scalar_max(out=dest, in0=bank, scalar1=0.0)

        w_raw = load("w_raw", w_rows)
        xa_raw = load("xa_raw", x_rows[:, :, 0:256])
        xb_raw = load("xb_raw", x_rows[:, :, 256:512])
        xc_raw = load("xc_raw", x_rows[:, :, 512:1024])

        vcopy = nc.vector.tensor_copy
        scopy = nc.scalar.copy

        wq = quantize("w", interleave("w_bf", vcopy, w_raw, 0, 256))

        a0 = interleave("a0_bf", vcopy, xa_raw, 0, 128)
        a1 = interleave("a1_bf", scopy, xa_raw, 128, 128)
        aq = [quantize("a0", a0), quantize("a1", a1)]
        for h in range(2):
            for t in range(2):
                for g in range(G):
                    c = 256 * t + 128 * h
                    multiply(wq, aq[h], 0, g, t, banks[g][0][:, c : c + N_TILE])
        bq = quantize("b", interleave("b_bf", vcopy, xb_raw, 0, 256))
        res_a = [sb.tile([P, 2, 256], F32, name="res_a%d" % g) for g in range(G)]
        for g, relu in ((0, relu_scalar), (1, relu_scalar), (3, relu_vector), (2, relu_scalar)):
            relu(res_a[g][:].rearrange("p t n -> p (t n)"), banks[g][0][:])
            nc.sync.dma_start(out=out_rows[:, 2 * g : 2 * g + 2, 0:256], in_=res_a[g][:])
        for h in range(2):
            for t in range(2):
                for g in range(G):
                    c = 256 * t + 128 * h
                    multiply(wq, bq, 128 * h, g, t, banks[g][1][:, c : c + N_TILE])
        c0 = interleave("c0_bf", vcopy, xc_raw, 0, 256)
        c1 = interleave("c1_bf", vcopy, xc_raw, 256, 256)
        cq = [quantize("c0", c0), quantize("c1", c1)]
        for pair in range(2):
            res_b = sb.tile([P, 4, 256], F32, name="res_b%d" % pair)
            for e in range(2):
                relu_scalar(res_b[:, 2 * e : 2 * e + 2, :].rearrange("p t n -> p (t n)"), banks[2 * pair + e][1][:])
            nc.sync.dma_start(out=out_rows[:, 4 * pair : 4 * pair + 4, 256:512], in_=res_b[:])
        for pair in range(2):
            for t in range(2):
                for q in range(4):
                    for g in (2 * pair, 2 * pair + 1):
                        multiply(wq, cq[q // 2], 128 * (q % 2), g, t, banks[g][t][:, 128 * q : 128 * (q + 1)])
        for g in range(G):
            res_c = sb.tile([P, 2, 512], F32, name="res_c%d" % g)
            relu_vector(res_c[:, 0, :], banks[g][0][:])
            relu_scalar(res_c[:, 1, :], banks[g][1][:])
            nc.sync.dma_start(out=out_rows[:, 2 * g : 2 * g + 2, 512:1024], in_=res_c[:])
